import numpy as np
import ml_dtypes


def mxq(x, axis, fmt="e4m3"):
    dtype, down = {"e4m3": (ml_dtypes.float8_e4m3fn, 7), "e5m2": (ml_dtypes.float8_e5m2, 14)}[fmt]
    v = np.moveaxis(np.asarray(x, np.float32).astype(ml_dtypes.bfloat16).astype(np.float64), axis, -1)
    blocks = v.reshape(v.shape[:-1] + (-1, 32))
    amax = np.abs(blocks).max(-1, keepdims=True)
    byte = np.maximum(np.where(amax > 0, np.frexp(amax)[1] - 1 + 127, 0) - down, 1)
    scale = np.exp2(byte - 127.0)
    codes = (blocks / scale).astype(np.float32).astype(dtype).astype(np.float64)
    return np.moveaxis((codes * scale).reshape(v.shape), -1, axis)


WIDE = False


def mx_kscale(k):
    if not WIDE:
        return np.ones(k)
    levels = np.array([30, -30])
    if k % 512:
        return np.exp2(np.random.permutation(np.resize(levels, k // 32))).repeat(32)
    a = np.empty((k // 512, 16))
    for p in range(k // 512):
        a[p, :8] = np.random.permutation(np.resize(levels, 8))
        for g in range(8):
            far = levels[np.abs(levels - a[p, g]) >= 10]
            a[p, g + 8] = far[np.random.randint(len(far))]
    return np.exp2(a.ravel()).repeat(32)


def f64(x):
    return np.asarray(x).astype(np.float64)


def striped(idx):
    return np.tile(np.asarray(idx).reshape(-1, 16).T, (8, 1)).astype(np.uint16)


def unstriped(offs):
    return offs[:16].T.reshape(-1).astype(np.int64)


E2M1 = np.array([0.0, 0.5, 1.0, 1.5, 2.0, 3.0, 4.0, 6.0, -0.0, -0.5, -1.0, -1.5, -2.0, -3.0, -4.0, -6.0])


def pack_weight(w, fmt):
    k, n = w.shape
    w = f64(np.asarray(w, np.float32).astype(ml_dtypes.bfloat16)).reshape(k // 32, 32, n)
    amax = np.abs(w).max(1)
    if fmt in ("e4m3", "e5m2"):
        byte = np.frexp(amax)[1] - 1 + 127 - (7 if fmt == "e4m3" else 14)
    else:
        mant, ex = np.frexp(amax / 6.0)
        byte = np.where(mant > 0.5, ex, ex - 1) + 127
    byte = np.clip(np.where(amax > 0, byte, 1), 1, 254)
    scaled = (w * np.exp2(127.0 - byte)[:, None, :]).reshape(k, n).astype(np.float32)
    by_word = np.ascontiguousarray(scaled.reshape(k // 512, 128, 4, n).transpose(0, 1, 3, 2))
    if fmt in ("e4m3", "e5m2"):
        words = by_word.astype(ml_dtypes.float8_e4m3fn if fmt == "e4m3" else ml_dtypes.float8_e5m2).view(np.uint8)
    else:
        c = by_word.astype(ml_dtypes.float4_e2m1fn).view(np.uint8) & 0xF
        words = (c[..., 0::2] | (c[..., 1::2] << 4)).reshape(k // 512, 128, 2 * n)
    return np.ascontiguousarray(words), np.ascontiguousarray(byte.astype(np.uint8).reshape(k // 512, 16, n))


def unpack_weight(words, scales, fmt):
    g, _, n = scales.shape
    words = np.ascontiguousarray(words).reshape(g, 128, n, -1)
    if fmt in ("e4m3", "e5m2"):
        vals = words.view(ml_dtypes.float8_e4m3fn if fmt == "e4m3" else ml_dtypes.float8_e5m2).astype(np.float64)
    else:
        nib = np.empty((g, 128, n, 4), np.uint8)
        nib[..., 0::2] = words & 0xF
        nib[..., 1::2] = words >> 4
        vals = E2M1[nib]
    vals = vals * np.repeat(np.exp2(scales.astype(np.float64) - 127.0), 8, axis=1)[..., None]
    return vals.transpose(0, 1, 3, 2).reshape(g * 512, n)


K, T, J, R, N = 1024, 1024, 384, 512, 256


def setup_inputs():
    n = np.random.standard_normal
    idx = np.random.permutation(T)[:J]
    idx2 = np.random.permutation(T)[:J]
    fk = mx_kscale(K)
    fr = mx_kscale(R)
    wp = pack_weight(n((K, R)) * 1 / np.sqrt(K) * fk[:, None] * fr, "e2m1")
    wbp = pack_weight(n((R, N)) * 1 / np.sqrt(R) / fr[:, None], "e5m2")
    return {
        "xf": (n((K, T))).astype(np.float32),
        "fk": (np.random.uniform(0.5, 2.0, (K, 1)) / fk[:, None]).astype(np.float32),
        "w_words": wp[0],
        "w_scales": wp[1],
        "wb_words": wbp[0],
        "wb_scales": wbp[1],
        "hi": (np.random.uniform(0.4, 1.2, (N, 1))).astype(np.float32),
        "rw": (np.random.uniform(0.5, 2.0, (1, J))).astype(np.float32),
        "offs": striped(idx),
        "offs2": striped(idx2),
    }


def reference(xf, fk, w_words, w_scales, wb_words, wb_scales, hi, rw, offs, offs2):
    idx = unstriped(offs)
    idx2 = unstriped(offs2)
    wu = unpack_weight(w_words, w_scales, "e2m1")
    wbu = unpack_weight(wb_words, wb_scales, "e5m2")
    u = (f64(xf)[:, idx] - f64(xf)[:, idx2]) * f64(fk)
    uq = mxq(u, 0, "e4m3")
    a = wu.T @ uq
    pk1 = np.max(a, axis=1, keepdims=True)
    hid = np.maximum(a - 0.4 * pk1, 0.0)
    hidq = mxq(hid, 0, "e4m3")
    p = wbu.T @ hidq
    y = np.minimum(p - f64(hi), 0.0) * f64(rw)
    return y

@@ -1,0 +1,226 @@
+from contextlib import ExitStack
+
+import concourse.mybir as mybir
+
+K, T, J, R, N = 1024, 1024, 384, 512, 256
+FLOPS = 2 * K * R * J + 2 * R * N * J
+
+F32 = mybir.dt.float32
+BF16 = mybir.dt.bfloat16
+I32 = mybir.dt.int32
+U32 = mybir.dt.uint32
+U16 = mybir.dt.uint16
+U8 = mybir.dt.uint8
+E4M3 = mybir.dt.float8_e4m3fn_x4
+E5M2 = mybir.dt.float8_e5m2_x4
+E2M1 = mybir.dt.float4_e2m1fn_x4
+ALU = mybir.AluOpType
+ACT = mybir.ActivationFunctionType
+
+P = 128
+PACK = 4
+PASSES = K // (P * PACK)
+PLANES = PASSES * PACK
+SL = 128
+SLICES = J // SL
+FUSED = 256
+
+
+def tile_list_pickgaps_peakgated_capped_kernel(tc, xf, fk, w_words, w_scales, wb_words, wb_scales, hi, rw, offs, offs2, out):
+    nc = tc.nc
+    with ExitStack() as ctx:
+        sb = ctx.enter_context(tc.tile_pool(name="sb", bufs=1))
+        ps = ctx.enter_context(tc.psum_pool(name="ps", bufs=1))
+
+        list1 = sb.tile([P, J // 16], U16, name="list1")
+        list2 = sb.tile([P, J // 16], U16, name="list2")
+        x = [sb.tile([P, T], F32, name="x%d" % i) for i in range(PLANES)]
+        w_raw = sb.tile([P, PASSES * 2 * R], U8, name="w_raw")
+        ws_raw = sb.tile([P, PASSES * R], U8, name="ws_raw")
+        w_dealt = sb.tile([P, PASSES * 2 * R], U8, name="w_dealt", align_bytes=64)
+        ws_dealt = sb.tile([P, PASSES * R], U8, name="ws_dealt", align_bytes=64)
+        wb = sb.tile([P, N], I32, name="wb", align_bytes=64)
+        wbs = sb.tile([P, N], U8, name="wbs", align_bytes=64)
+        fk_sb = sb.tile([P, PLANES], F32, name="fk_sb")
+        hi_sb = sb.tile([P, N // P], F32, name="hi_sb")
+        rw_sb = sb.tile([P, J], F32, name="rw_sb")
+
+        nc.vector.memset(ws_raw[:].bitcast(U32), 0)
+        nc.vector.memset(wbs[:].bitcast(U32), 0)
+
+        x_rows = xf.rearrange("(a p t) c -> a t p c", p=P, t=PACK)
+
+        def load_plane(i):
+            nc.sync.dma_start(x[i][:], x_rows[i // PACK, i % PACK])
+
+        nc.sync.dma_start(list2[:], offs2)
+        nc.sync.dma_start(list1[:], offs)
+        load_plane(0)
+        nc.sync.dma_start(
+            fk_sb[:].rearrange("p (a t) -> p a t", a=PASSES),
+            fk.rearrange("(a p t) o -> p a (t o)", p=P, t=PACK),
+        )
+        load_plane(1)
+        ws_rows = w_scales.bitcast(I32).rearrange("a q c -> q a c")
+        for q in range(4):
+            nc.sync.dma_start(
+                ws_raw[32 * q : 32 * q + 4, :].bitcast(I32).rearrange("p (a c) -> p a c", a=PASSES),
+                ws_rows[4 * q : 4 * q + 4],
+            )
+        nc.sync.dma_start(
+            w_raw[:].bitcast(I32).rearrange("p (a c) -> p a c", a=PASSES),
+            w_words.bitcast(I32).rearrange("a p c -> p a c"),
+        )
+        for i in range(2, PLANES):
+            load_plane(i)
+        nc.sync.dma_start(wb[:], wb_words[0].rearrange("p n t -> p (n t)").bitcast(I32))
+        for q in range(4):
+            nc.sync.dma_start(wbs[32 * q : 32 * q + 4, :].bitcast(I32), wb_scales[0].bitcast(I32)[4 * q : 4 * q + 4, :])
+        with nc.allow_non_contiguous_dma(reason="one bound for each partition"):
+            nc.sync.dma_start(hi_sb[:], hi.rearrange("(c p) o -> p (c o)", p=P))
+        nc.sync.dma_start(rw_sb[:], rw[0].partition_broadcast(P))
+
+        def entries(tile, lo, hi_col):
+            return tile[:, lo // 16 : hi_col // 16]
+
+        second = [sb.tile([P, J], F32, name="second%d" % i) for i in range(PLANES)]
+        first = [sb.tile([P, J - FUSED], F32, name="first%d" % i) for i in range(PLANES)]
+        gap = [sb.tile([P, J], F32, name="gap%d" % i) for i in range(PLANES)]
+        u_pairs = [sb.tile([P, PACK * J], BF16, name="u_pairs%d" % a) for a in range(PASSES)]
+        u_woven = [sb.tile([P, PACK * J], BF16, name="u_woven%d" % a, align_bytes=64) for a in range(PASSES)]
+        u_codes = [sb.tile([P, J], U32, name="u_codes%d" % a, align_bytes=64) for a in range(PASSES)]
+        u_scales = [sb.tile([P, J], U8, name="u_scales%d" % a, align_bytes=64) for a in range(PASSES)]
+        acc = [ps.tile([P, J], F32, name="acc%d" % t) for t in range(PACK)]
+
+        def pair_view(pairs, t, lo, hi_col):
+            base = (t // 2) * 2 * J + t % 2
+            return pairs[:, base + 2 * lo : base + 2 * hi_col - 1 : 2]
+
+        def gather_second(i, lo, hi_col):
+            nc.scalar.activation(second[i][:, lo:hi_col], x[i][:].indirect(entries(list2, lo, hi_col)), ACT.Copy)
+
+        def gather_first(i):
+            nc.scalar.activation(first[i][:], x[i][:].indirect(entries(list1, FUSED, J)), ACT.Copy)
+
+        def gather_subtract(i, lo, hi_col):
+            nc.vector.tensor_tensor(
+                gap[i][:, lo:hi_col], x[i][:].indirect(entries(list1, lo, hi_col)), second[i][:, lo:hi_col], ALU.subtract
+            )
+
+        def subtract(i):
+            nc.vector.tensor_tensor(gap[i][:, FUSED:J], first[i][:], second[i][:, FUSED:J], ALU.subtract)
+
+        def scale_round(i, lo, hi_col):
+            nc.vector.tensor_scalar(
+                pair_view(u_pairs[i // PACK], i % PACK, lo, hi_col), gap[i][:, lo:hi_col], fk_sb[:, i : i + 1], None, ALU.mult
+            )
+
+        def weave(on_scalar, woven, pairs, lo, hi_col):
+            word = U32 if on_scalar else I32
+            dst = woven[:].bitcast(word)[:, 2 * lo : 2 * hi_col].rearrange("p (c i h) -> p c h i", i=4, h=2)
+            src = pairs[:].bitcast(word).rearrange("p (h c i) -> p c h i", h=2, i=4)[:, lo // 4 : hi_col // 4]
+            if on_scalar:
+                nc.scalar.copy(dst, src)
+            else:
+                nc.vector.tensor_copy(dst, src)
+
+        def quantise(codes, scales, woven, lo, hi_col):
+            nc.vector.quantize_mx(
+                out=codes[:, lo:hi_col].bitcast(E4M3), scales=scales[:, lo:hi_col], in_=woven[:, PACK * lo : PACK * hi_col]
+            )
+
+        def first_product(a, lo, hi_col):
+            for t in range(PACK):
+                col = a * R + t * P
+                nc.tensor.matmul_mx(
+                    out=acc[t][:, lo:hi_col],
+                    lhsT=w_dealt[:, 2 * col : 2 * (col + P)].bitcast(E2M1),
+                    lhsT_scale=ws_dealt[:, col : col + P],
+                    rhs=u_codes[a][:, lo:hi_col].bitcast(E4M3),
+                    rhs_scale=u_scales[a][:, lo:hi_col],
+                    start=(a == 0 and lo == 0),
+                    stop=(a == PASSES - 1 and hi_col == J),
+                )
+
+        for i in range(PLANES - 1):
+            gather_second(i, 0, J)
+            gather_first(i)
+            gather_subtract(i, 0, FUSED)
+            subtract(i)
+            scale_round(i, 0, FUSED)
+            scale_round(i, FUSED, J)
+            if i == 0:
+                nc.vector.tensor_copy(
+                    ws_dealt[:].rearrange("p (a t m) -> p a t m", a=PASSES, t=PACK),
+                    ws_raw[:].rearrange("p (a m t) -> p a t m", a=PASSES, t=PACK),
+                )
+            if i == 1:
+                nc.vector.tensor_copy(
+                    w_dealt[:].bitcast(U16).rearrange("p (a t m) -> p a t m", a=PASSES, t=PACK),
+                    w_raw[:].bitcast(U16).rearrange("p (a m t) -> p a t m", a=PASSES, t=PACK),
+                )
+            if i == PACK - 1:
+                weave(False, u_woven[0], u_pairs[0], 0, J)
+            if i == PACK:
+                quantise(u_codes[0], u_scales[0], u_woven[0], 0, J)
+                first_product(0, 0, FUSED)
+                first_product(0, FUSED, J)
+
+        last = PLANES - 1
+        for s in range(SLICES):
+            gather_second(last, s * SL, (s + 1) * SL)
+        gather_first(last)
+        gather_subtract(last, 0, SL)
+        gather_subtract(last, SL, 2 * SL)
+        scale_round(last, 0, SL)
+        subtract(last)
+        scale_round(last, SL, 2 * SL)
+        scale_round(last, 2 * SL, J)
+        for s in range(SLICES):
+            weave(s < SLICES - 1, u_woven[1], u_pairs[1], s * SL, (s + 1) * SL)
+        for s in range(SLICES):
+            quantise(u_codes[1], u_scales[1], u_woven[1], s * SL, (s + 1) * SL)
+            first_product(1, s * SL, (s + 1) * SL)
+
+        scaled = [sb.tile([P, J], F32, name="scaled%d" % t) for t in range(PACK)]
+        cut = [sb.tile([P, 1], F32, name="cut%d" % t) for t in range(PACK)]
+        h_pairs = sb.tile([P, PACK * J], BF16, name="h_pairs")
+        h_woven = sb.tile([P, PACK * J], BF16, name="h_woven", align_bytes=64)
+        h_codes = sb.tile([P, J], U32, name="h_codes", align_bytes=64)
+        h_scales = sb.tile([P, J], U8, name="h_scales", align_bytes=64)
+        for t in range(PACK):
+            nc.vector.tensor_scalar(scaled[t][:], acc[t][:], -0.4, None, ALU.mult, ALU.min, accum_out=cut[t][:])
+            width = J if t < 2 else J - SL
+            nc.scalar.activation(
+                pair_view(h_pairs, t, J - width, J), acc[t][:, J - width : J], ACT.Relu, bias=cut[t][:]
+            )
+        for t in (3, 2):
+            nc.vector.tensor_scalar(pair_view(h_pairs, t, 0, SL), acc[t][:, 0:SL], cut[t][:], 0.0, ALU.add, ALU.max)
+
+        prod = [ps.tile([P, N // P, SL], F32, name="prod%d" % s) for s in range(SLICES)]
+        under = [sb.tile([P, N // P, SL], F32, name="under%d" % s) for s in range(SLICES)]
+        result = [sb.tile([P, N // P, SL], F32, name="result%d" % s) for s in range(SLICES)]
+        out_rows = out.rearrange("(c p) j -> p c j", p=P)
+        for s in range(SLICES):
+            weave(False, h_woven, h_pairs, s * SL, (s + 1) * SL)
+        for s in range(SLICES):
+            lo, hi_col = s * SL, (s + 1) * SL
+            quantise(h_codes, h_scales, h_woven, lo, hi_col)
+            for c in range(N // P):
+                nc.tensor.matmul_mx(
+                    out=prod[s][:, c, :],
+                    lhsT=wb[:, c * P : (c + 1) * P].bitcast(E5M2),
+                    lhsT_scale=wbs[:, c * P : (c + 1) * P],
+                    rhs=h_codes[:, lo:hi_col].bitcast(E4M3),
+                    rhs_scale=h_scales[:, lo:hi_col],
+                    start=True,
+                    stop=True,
+                )
+        for s in range(SLICES):
+            lo, hi_col = s * SL, (s + 1) * SL
+            for c in range(N // P):
+                nc.scalar.activation(under[s][:, c, :], prod[s][:, c, :], ACT.Relu, bias=hi_sb[:, c : c + 1], scale=-1.0)
+            nc.vector.scalar_tensor_tensor(
+                result[s][:], under[s][:], -1.0, rw_sb[:, lo:hi_col].unsqueeze(1).to_broadcast([P, N // P, SL]), ALU.mult, ALU.mult
+            )
+            nc.sync.dma_start(out_rows[:, :, lo:hi_col], result[s][:])

@@ -23,7 +23,8 @@ PASSES = K // (P * PACK)
 PLANES = PASSES * PACK
 SL = 128
 SLICES = J // SL
-FUSED = 256
+FUSED = 192
+WIDE = 256
 
 
 def tile_list_pickgaps_peakgated_capped_kernel(tc, xf, fk, w_words, w_scales, wb_words, wb_scales, hi, rw, offs, offs2, out):
@@ -57,6 +58,10 @@ def tile_list_pickgaps_peakgated_capped_kernel(tc, xf, fk, w_words, w_scales, wb
         nc.sync.dma_start(list1[:], offs)
         load_plane(0)
         nc.sync.dma_start(
+            w_raw[:].bitcast(I32).rearrange("p (a c) -> p a c", a=PASSES),
+            w_words.bitcast(I32).rearrange("a p c -> p a c"),
+        )
+        nc.gpsimd.dma_start(
             fk_sb[:].rearrange("p (a t) -> p a t", a=PASSES),
             fk.rearrange("(a p t) o -> p a (t o)", p=P, t=PACK),
         )
@@ -67,10 +72,6 @@ def tile_list_pickgaps_peakgated_capped_kernel(tc, xf, fk, w_words, w_scales, wb
                 ws_raw[32 * q : 32 * q + 4, :].bitcast(I32).rearrange("p (a c) -> p a c", a=PASSES),
                 ws_rows[4 * q : 4 * q + 4],
             )
-        nc.sync.dma_start(
-            w_raw[:].bitcast(I32).rearrange("p (a c) -> p a c", a=PASSES),
-            w_words.bitcast(I32).rearrange("a p c -> p a c"),
-        )
         for i in range(2, PLANES):
             load_plane(i)
         nc.sync.dma_start(wb[:], wb_words[0].rearrange("p n t -> p (n t)").bitcast(I32))
@@ -83,14 +84,15 @@ def tile_list_pickgaps_peakgated_capped_kernel(tc, xf, fk, w_words, w_scales, wb
         def entries(tile, lo, hi_col):
             return tile[:, lo // 16 : hi_col // 16]
 
-        second = [sb.tile([P, J], F32, name="second%d" % i) for i in range(PLANES)]
-        first = [sb.tile([P, J - FUSED], F32, name="first%d" % i) for i in range(PLANES)]
+        second = [sb.tile([P, J], F32, name="second%d" % i, tag="second%d" % i, align_bytes=64) for i in range(PLANES)]
+        first = [sb.tile([P, J], F32, name="first%d" % i) for i in range(PLANES)]
         gap = [sb.tile([P, J], F32, name="gap%d" % i) for i in range(PLANES)]
         u_pairs = [sb.tile([P, PACK * J], BF16, name="u_pairs%d" % a) for a in range(PASSES)]
         u_woven = [sb.tile([P, PACK * J], BF16, name="u_woven%d" % a, align_bytes=64) for a in range(PASSES)]
-        u_codes = [sb.tile([P, J], U32, name="u_codes%d" % a, align_bytes=64) for a in range(PASSES)]
+        u_codes = [None, sb.tile([P, J], U32, name="u_codes1", align_bytes=64)]
         u_scales = [sb.tile([P, J], U8, name="u_scales%d" % a, align_bytes=64) for a in range(PASSES)]
         acc = [ps.tile([P, J], F32, name="acc%d" % t) for t in range(PACK)]
+        acc_head = ps.tile([P, SL], F32, name="acc_head")
 
         def pair_view(pairs, t, lo, hi_col):
             base = (t // 2) * 2 * J + t % 2
@@ -99,88 +101,92 @@ def tile_list_pickgaps_peakgated_capped_kernel(tc, xf, fk, w_words, w_scales, wb
         def gather_second(i, lo, hi_col):
             nc.scalar.activation(second[i][:, lo:hi_col], x[i][:].indirect(entries(list2, lo, hi_col)), ACT.Copy)
 
-        def gather_first(i):
-            nc.scalar.activation(first[i][:], x[i][:].indirect(entries(list1, FUSED, J)), ACT.Copy)
+        def gather_first(i, lo, hi_col):
+            nc.scalar.activation(first[i][:, lo:hi_col], x[i][:].indirect(entries(list1, lo, hi_col)), ACT.Copy)
 
         def gather_subtract(i, lo, hi_col):
             nc.vector.tensor_tensor(
                 gap[i][:, lo:hi_col], x[i][:].indirect(entries(list1, lo, hi_col)), second[i][:, lo:hi_col], ALU.subtract
             )
 
-        def subtract(i):
-            nc.vector.tensor_tensor(gap[i][:, FUSED:J], first[i][:], second[i][:, FUSED:J], ALU.subtract)
+        def subtract(i, lo, hi_col):
+            nc.vector.tensor_tensor(gap[i][:, lo:hi_col], first[i][:, lo:hi_col], second[i][:, lo:hi_col], ALU.subtract)
 
         def scale_round(i, lo, hi_col):
             nc.vector.tensor_scalar(
                 pair_view(u_pairs[i // PACK], i % PACK, lo, hi_col), gap[i][:, lo:hi_col], fk_sb[:, i : i + 1], None, ALU.mult
             )
 
-        def weave(on_scalar, woven, pairs, lo, hi_col):
-            word = U32 if on_scalar else I32
-            dst = woven[:].bitcast(word)[:, 2 * lo : 2 * hi_col].rearrange("p (c i h) -> p c h i", i=4, h=2)
-            src = pairs[:].bitcast(word).rearrange("p (h c i) -> p c h i", h=2, i=4)[:, lo // 4 : hi_col // 4]
-            if on_scalar:
-                nc.scalar.copy(dst, src)
-            else:
-                nc.vector.tensor_copy(dst, src)
+        def weave(woven, pairs, lo, hi_col):
+            nc.vector.tensor_copy(
+                woven[:].bitcast(I32)[:, 2 * lo : 2 * hi_col].rearrange("p (j h) -> p j h", h=2),
+                pairs[:].bitcast(I32).rearrange("p (h j) -> p j h", h=2)[:, lo:hi_col],
+            )
 
         def quantise(codes, scales, woven, lo, hi_col):
             nc.vector.quantize_mx(
                 out=codes[:, lo:hi_col].bitcast(E4M3), scales=scales[:, lo:hi_col], in_=woven[:, PACK * lo : PACK * hi_col]
             )
 
-        def first_product(a, lo, hi_col):
-            for t in range(PACK):
-                col = a * R + t * P
-                nc.tensor.matmul_mx(
-                    out=acc[t][:, lo:hi_col],
-                    lhsT=w_dealt[:, 2 * col : 2 * (col + P)].bitcast(E2M1),
-                    lhsT_scale=ws_dealt[:, col : col + P],
-                    rhs=u_codes[a][:, lo:hi_col].bitcast(E4M3),
-                    rhs_scale=u_scales[a][:, lo:hi_col],
-                    start=(a == 0 and lo == 0),
-                    stop=(a == PASSES - 1 and hi_col == J),
-                )
+        peak_order = (2, 0, 1, 3)
+
+        def product_pass(a, t, bank, lo, hi_col, opens, closes):
+            col = a * R + t * P
+            nc.tensor.matmul_mx(
+                out=bank,
+                lhsT=w_dealt[:, 2 * col : 2 * (col + P)].bitcast(E2M1),
+                lhsT_scale=ws_dealt[:, col : col + P],
+                rhs=u_codes[a][:, lo:hi_col].bitcast(E4M3),
+                rhs_scale=u_scales[a][:, lo:hi_col],
+                start=(a == 0 and opens),
+                stop=(a == PASSES - 1 and closes),
+            )
+
+        def first_product(a):
+            product_pass(a, 3, acc_head[:], 0, SL, True, True)
+            for t in peak_order[:3]:
+                product_pass(a, t, acc[t][:, 0:WIDE], 0, WIDE, True, False)
+                product_pass(a, t, acc[t][:, WIDE:J], WIDE, J, False, True)
+            product_pass(a, 3, acc[3][:, SL:J], SL, J, True, True)
 
         for i in range(PLANES - 1):
             gather_second(i, 0, J)
-            gather_first(i)
+            gather_first(i, FUSED, J)
             gather_subtract(i, 0, FUSED)
-            subtract(i)
+            subtract(i, FUSED, J)
             scale_round(i, 0, FUSED)
             scale_round(i, FUSED, J)
             if i == 0:
                 nc.vector.tensor_copy(
-                    ws_dealt[:].rearrange("p (a t m) -> p a t m", a=PASSES, t=PACK),
-                    ws_raw[:].rearrange("p (a m t) -> p a t m", a=PASSES, t=PACK),
-                )
-            if i == 1:
-                nc.vector.tensor_copy(
                     w_dealt[:].bitcast(U16).rearrange("p (a t m) -> p a t m", a=PASSES, t=PACK),
                     w_raw[:].bitcast(U16).rearrange("p (a m t) -> p a t m", a=PASSES, t=PACK),
                 )
+            if i == 1:
+                nc.vector.tensor_copy(
+                    ws_dealt[:].rearrange("p (a t m) -> p a t m", a=PASSES, t=PACK),
+                    ws_raw[:].rearrange("p (a m t) -> p a t m", a=PASSES, t=PACK),
+                )
             if i == PACK - 1:
-                weave(False, u_woven[0], u_pairs[0], 0, J)
-            if i == PACK:
+                weave(u_woven[0], u_pairs[0], 0, J)
+            if i == PACK + 1:
+                u_codes[0] = sb.tile([P, J], U32, name="u_codes0", tag="second%d" % i, align_bytes=64)
                 quantise(u_codes[0], u_scales[0], u_woven[0], 0, J)
-                first_product(0, 0, FUSED)
-                first_product(0, FUSED, J)
+                first_product(0)
 
         last = PLANES - 1
-        for s in range(SLICES):
-            gather_second(last, s * SL, (s + 1) * SL)
-        gather_first(last)
+        gather_second(last, 0, SL)
         gather_subtract(last, 0, SL)
-        gather_subtract(last, SL, 2 * SL)
-        scale_round(last, 0, SL)
-        subtract(last)
-        scale_round(last, SL, 2 * SL)
-        scale_round(last, 2 * SL, J)
+        for s in range(1, SLICES):
+            gather_second(last, s * SL, (s + 1) * SL)
+            gather_first(last, s * SL, (s + 1) * SL)
+            subtract(last, s * SL, (s + 1) * SL)
         for s in range(SLICES):
-            weave(s < SLICES - 1, u_woven[1], u_pairs[1], s * SL, (s + 1) * SL)
-        for s in range(SLICES):
-            quantise(u_codes[1], u_scales[1], u_woven[1], s * SL, (s + 1) * SL)
-            first_product(1, s * SL, (s + 1) * SL)
+            scale_round(last, s * SL, (s + 1) * SL)
+        for lo, hi_col in ((0, WIDE), (WIDE, J)):
+            weave(u_woven[1], u_pairs[1], lo, hi_col)
+        for lo, hi_col in ((0, WIDE), (WIDE, J)):
+            quantise(u_codes[1], u_scales[1], u_woven[1], lo, hi_col)
+        first_product(1)
 
         scaled = [sb.tile([P, J], F32, name="scaled%d" % t) for t in range(PACK)]
         cut = [sb.tile([P, 1], F32, name="cut%d" % t) for t in range(PACK)]
@@ -188,22 +194,28 @@ def tile_list_pickgaps_peakgated_capped_kernel(tc, xf, fk, w_words, w_scales, wb
         h_woven = sb.tile([P, PACK * J], BF16, name="h_woven", align_bytes=64)
         h_codes = sb.tile([P, J], U32, name="h_codes", align_bytes=64)
         h_scales = sb.tile([P, J], U8, name="h_scales", align_bytes=64)
-        for t in range(PACK):
+        cut_head = sb.tile([P, 1], F32, name="cut_head")
+        nc.vector.tensor_scalar(scaled[3][:, 0:SL], acc_head[:], -0.4, None, ALU.mult, ALU.min, accum_out=cut_head[:])
+        for t in peak_order[:3]:
             nc.vector.tensor_scalar(scaled[t][:], acc[t][:], -0.4, None, ALU.mult, ALU.min, accum_out=cut[t][:])
-            width = J if t < 2 else J - SL
+            lo = 0 if t < 2 else SL
+            nc.scalar.activation(pair_view(h_pairs, t, lo, J), acc[t][:, lo:J], ACT.Relu, bias=cut[t][:])
+        nc.vector.tensor_scalar(scaled[3][:, SL:J], acc[3][:, SL:J], -0.4, cut_head[:], ALU.mult, ALU.min, accum_out=cut[3][:])
+        nc.vector.tensor_scalar(pair_view(h_pairs, 2, 0, SL), acc[2][:, 0:SL], cut[2][:], 0.0, ALU.add, ALU.max)
+        nc.vector.tensor_scalar(pair_view(h_pairs, 3, 0, SL), acc_head[:], cut[3][:], 0.0, ALU.add, ALU.max)
+        for s in range(1, SLICES):
             nc.scalar.activation(
-                pair_view(h_pairs, t, J - width, J), acc[t][:, J - width : J], ACT.Relu, bias=cut[t][:]
+                pair_view(h_pairs, 3, s * SL, (s + 1) * SL), acc[3][:, s * SL : (s + 1) * SL], ACT.Relu, bias=cut[3][:]
             )
-        for t in (3, 2):
-            nc.vector.tensor_scalar(pair_view(h_pairs, t, 0, SL), acc[t][:, 0:SL], cut[t][:], 0.0, ALU.add, ALU.max)
 
         prod = [ps.tile([P, N // P, SL], F32, name="prod%d" % s) for s in range(SLICES)]
         under = [sb.tile([P, N // P, SL], F32, name="under%d" % s) for s in range(SLICES)]
         result = [sb.tile([P, N // P, SL], F32, name="result%d" % s) for s in range(SLICES)]
         out_rows = out.rearrange("(c p) j -> p c j", p=P)
-        for s in range(SLICES):
-            weave(False, h_woven, h_pairs, s * SL, (s + 1) * SL)
-        for s in range(SLICES):
+        slice_order = (0, 1, 2)
+        for s in slice_order:
+            weave(h_woven, h_pairs, s * SL, (s + 1) * SL)
+        for s in slice_order:
             lo, hi_col = s * SL, (s + 1) * SL
             quantise(h_codes, h_scales, h_woven, lo, hi_col)
             for c in range(N // P):
@@ -216,7 +228,7 @@ def tile_list_pickgaps_peakgated_capped_kernel(tc, xf, fk, w_words, w_scales, wb
                     start=True,
                     stop=True,
                 )
-        for s in range(SLICES):
+        for s in slice_order:
             lo, hi_col = s * SL, (s + 1) * SL
             for c in range(N // P):
                 nc.scalar.activation(under[s][:, c, :], prod[s][:, c, :], ACT.Relu, bias=hi_sb[:, c : c + 1], scale=-1.0)

@@ -49,6 +49,11 @@ def tile_list_pickgaps_peakgated_capped_kernel(tc, xf, fk, w_words, w_scales, wb
         nc.vector.memset(ws_raw[:].bitcast(U32), 0)
         nc.vector.memset(wbs[:].bitcast(U32), 0)
 
+        warm_in = sb.tile([P, 1], F32, name="warm_in")
+        warm_out = sb.tile([P, 1], F32, name="warm_out")
+        nc.gpsimd.memset(warm_in[:], 0.0)
+        nc.scalar.activation(warm_out[:], warm_in[:], ACT.Copy)
+
         x_rows = xf.rearrange("(a p t) c -> a t p c", p=P, t=PACK)
 
         def load_plane(i):

@@ -23,7 +23,7 @@ PASSES = K // (P * PACK)
 PLANES = PASSES * PACK
 SL = 128
 SLICES = J // SL
-FUSED = 192
+FUSED = 256
 WIDE = 256
 
 
@@ -60,8 +60,8 @@ def tile_list_pickgaps_peakgated_capped_kernel(tc, xf, fk, w_words, w_scales, wb
             nc.sync.dma_start(x[i][:], x_rows[i // PACK, i % PACK])
 
         nc.sync.dma_start(list2[:], offs2)
-        nc.sync.dma_start(list1[:], offs)
         load_plane(0)
+        nc.sync.dma_start(list1[:], offs)
         nc.sync.dma_start(
             w_raw[:].bitcast(I32).rearrange("p (a c) -> p a c", a=PASSES),
             w_words.bitcast(I32).rearrange("a p c -> p a c"),

@@ -21,29 +21,37 @@ P = 128
 PACK = 4
 PASSES = K // (P * PACK)
 PLANES = PASSES * PACK
-SL = 128
-SLICES = J // SL
-FUSED = 256
-WIDE = 256
+QUADRANTS = 4
+ENTRIES_PER_COLUMN = 16
+SLICE = 128
+SLICES = J // SLICE
+WIDE = 2 * SLICE
+OUT_TILES = N // P
+PEAK_SHARE = 0.4
+
+FUSED = (256, 128)
+
+PEAK_ORDER = (2, 0, 1, 3)
 
 
-def tile_list_pickgaps_peakgated_capped_kernel(tc, xf, fk, w_words, w_scales, wb_words, wb_scales, hi, rw, offs, offs2, out):
+def tile_list_pickgaps_peakgated_capped_kernel(
+    tc, xf, fk, w_words, w_scales, wb_words, wb_scales, hi, rw, offs, offs2, out
+):
     nc = tc.nc
     with ExitStack() as ctx:
         sb = ctx.enter_context(tc.tile_pool(name="sb", bufs=1))
         ps = ctx.enter_context(tc.psum_pool(name="ps", bufs=1))
 
-        list1 = sb.tile([P, J // 16], U16, name="list1")
-        list2 = sb.tile([P, J // 16], U16, name="list2")
+        list1 = sb.tile([P, J // ENTRIES_PER_COLUMN], U16, name="list1")
+        list2 = sb.tile([P, J // ENTRIES_PER_COLUMN], U16, name="list2")
         x = [sb.tile([P, T], F32, name="x%d" % i) for i in range(PLANES)]
         w_raw = sb.tile([P, PASSES * 2 * R], U8, name="w_raw")
         ws_raw = sb.tile([P, PASSES * R], U8, name="ws_raw")
         w_dealt = sb.tile([P, PASSES * 2 * R], U8, name="w_dealt", align_bytes=64)
-        ws_dealt = sb.tile([P, PASSES * R], U8, name="ws_dealt", align_bytes=64)
         wb = sb.tile([P, N], I32, name="wb", align_bytes=64)
         wbs = sb.tile([P, N], U8, name="wbs", align_bytes=64)
-        fk_sb = sb.tile([P, PLANES], F32, name="fk_sb")
-        hi_sb = sb.tile([P, N // P], F32, name="hi_sb")
+        fk_sb = [sb.tile([P, PACK], F32, name="fk_sb%d" % a) for a in range(PASSES)]
+        hi_sb = sb.tile([P, OUT_TILES], F32, name="hi_sb")
         rw_sb = sb.tile([P, J], F32, name="rw_sb")
 
         nc.vector.memset(ws_raw[:].bitcast(U32), 0)
@@ -59,139 +67,142 @@ def tile_list_pickgaps_peakgated_capped_kernel(tc, xf, fk, w_words, w_scales, wb
         def load_plane(i):
             nc.sync.dma_start(x[i][:], x_rows[i // PACK, i % PACK])
 
+        fk_rows = fk.rearrange("(a p t) o -> a p (t o)", p=P, t=PACK)
         nc.sync.dma_start(list2[:], offs2)
         load_plane(0)
         nc.sync.dma_start(list1[:], offs)
+        nc.sync.dma_start(fk_sb[0][:], fk_rows[0])
         nc.sync.dma_start(
             w_raw[:].bitcast(I32).rearrange("p (a c) -> p a c", a=PASSES),
             w_words.bitcast(I32).rearrange("a p c -> p a c"),
         )
-        nc.gpsimd.dma_start(
-            fk_sb[:].rearrange("p (a t) -> p a t", a=PASSES),
-            fk.rearrange("(a p t) o -> p a (t o)", p=P, t=PACK),
-        )
         load_plane(1)
+        load_plane(2)
         ws_rows = w_scales.bitcast(I32).rearrange("a q c -> q a c")
-        for q in range(4):
+        for q in range(QUADRANTS):
             nc.sync.dma_start(
                 ws_raw[32 * q : 32 * q + 4, :].bitcast(I32).rearrange("p (a c) -> p a c", a=PASSES),
                 ws_rows[4 * q : 4 * q + 4],
             )
-        for i in range(2, PLANES):
+        load_plane(3)
+        nc.sync.dma_start(fk_sb[1][:], fk_rows[1])
+        for i in range(PACK, PLANES):
             load_plane(i)
         nc.sync.dma_start(wb[:], wb_words[0].rearrange("p n t -> p (n t)").bitcast(I32))
-        for q in range(4):
+        for q in range(QUADRANTS):
             nc.sync.dma_start(wbs[32 * q : 32 * q + 4, :].bitcast(I32), wb_scales[0].bitcast(I32)[4 * q : 4 * q + 4, :])
         with nc.allow_non_contiguous_dma(reason="one bound for each partition"):
             nc.sync.dma_start(hi_sb[:], hi.rearrange("(c p) o -> p (c o)", p=P))
         nc.sync.dma_start(rw_sb[:], rw[0].partition_broadcast(P))
 
-        def entries(tile, lo, hi_col):
-            return tile[:, lo // 16 : hi_col // 16]
-
-        second = [sb.tile([P, J], F32, name="second%d" % i, tag="second%d" % i, align_bytes=64) for i in range(PLANES)]
+        second = [
+            sb.tile([P, J], F32, name="second%d" % i, tag="second%d" % i, align_bytes=64) for i in range(PLANES)
+        ]
         first = [sb.tile([P, J], F32, name="first%d" % i) for i in range(PLANES)]
         gap = [sb.tile([P, J], F32, name="gap%d" % i) for i in range(PLANES)]
         u_pairs = [sb.tile([P, PACK * J], BF16, name="u_pairs%d" % a) for a in range(PASSES)]
         u_woven = [sb.tile([P, PACK * J], BF16, name="u_woven%d" % a, align_bytes=64) for a in range(PASSES)]
-        u_codes = [None, sb.tile([P, J], U32, name="u_codes1", align_bytes=64)]
+        u_codes_last = sb.tile([P, J], U32, name="u_codes1", align_bytes=64)
         u_scales = [sb.tile([P, J], U8, name="u_scales%d" % a, align_bytes=64) for a in range(PASSES)]
         acc = [ps.tile([P, J], F32, name="acc%d" % t) for t in range(PACK)]
-        acc_head = ps.tile([P, SL], F32, name="acc_head")
+        acc_head = ps.tile([P, SLICE], F32, name="acc_head")
 
-        def pair_view(pairs, t, lo, hi_col):
+        def entries(list_tile, lo, end):
+            return list_tile[:, lo // ENTRIES_PER_COLUMN : end // ENTRIES_PER_COLUMN]
+
+        def pair_view(pairs, t, lo, end):
             base = (t // 2) * 2 * J + t % 2
-            return pairs[:, base + 2 * lo : base + 2 * hi_col - 1 : 2]
+            return pairs[:, base + 2 * lo : base + 2 * end - 1 : 2]
 
-        def gather_second(i, lo, hi_col):
-            nc.scalar.activation(second[i][:, lo:hi_col], x[i][:].indirect(entries(list2, lo, hi_col)), ACT.Copy)
+        def gather_second(i, lo, end):
+            nc.scalar.activation(second[i][:, lo:end], x[i][:].indirect(entries(list2, lo, end)), ACT.Copy)
 
-        def gather_first(i, lo, hi_col):
-            nc.scalar.activation(first[i][:, lo:hi_col], x[i][:].indirect(entries(list1, lo, hi_col)), ACT.Copy)
+        def gather_first(i, lo, end):
+            nc.scalar.activation(first[i][:, lo:end], x[i][:].indirect(entries(list1, lo, end)), ACT.Copy)
 
-        def gather_subtract(i, lo, hi_col):
+        def gather_subtract(i, lo, end):
             nc.vector.tensor_tensor(
-                gap[i][:, lo:hi_col], x[i][:].indirect(entries(list1, lo, hi_col)), second[i][:, lo:hi_col], ALU.subtract
+                gap[i][:, lo:end], x[i][:].indirect(entries(list1, lo, end)), second[i][:, lo:end], ALU.subtract
             )
 
-        def subtract(i, lo, hi_col):
-            nc.vector.tensor_tensor(gap[i][:, lo:hi_col], first[i][:, lo:hi_col], second[i][:, lo:hi_col], ALU.subtract)
+        def subtract(i, lo, end):
+            nc.vector.tensor_tensor(gap[i][:, lo:end], first[i][:, lo:end], second[i][:, lo:end], ALU.subtract)
 
-        def scale_round(i, lo, hi_col):
+        def scale_round(i, lo, end):
+            a, t = divmod(i, PACK)
             nc.vector.tensor_scalar(
-                pair_view(u_pairs[i // PACK], i % PACK, lo, hi_col), gap[i][:, lo:hi_col], fk_sb[:, i : i + 1], None, ALU.mult
+                pair_view(u_pairs[a], t, lo, end), gap[i][:, lo:end], fk_sb[a][:, t : t + 1], None, ALU.mult
             )
 
-        def weave(woven, pairs, lo, hi_col):
+        def deal_columns(dealt, raw):
             nc.vector.tensor_copy(
-                woven[:].bitcast(I32)[:, 2 * lo : 2 * hi_col].rearrange("p (j h) -> p j h", h=2),
-                pairs[:].bitcast(I32).rearrange("p (h j) -> p j h", h=2)[:, lo:hi_col],
+                dealt.rearrange("p (a t m) -> p a t m", a=PASSES, t=PACK),
+                raw.rearrange("p (a m t) -> p a t m", a=PASSES, t=PACK),
             )
 
-        def quantise(codes, scales, woven, lo, hi_col):
+        def weave(woven, pairs, lo, end):
+            nc.vector.tensor_copy(
+                woven[:].bitcast(I32)[:, 2 * lo : 2 * end].rearrange("p (j h) -> p j h", h=2),
+                pairs[:].bitcast(I32).rearrange("p (h j) -> p j h", h=2)[:, lo:end],
+            )
+
+        def quantise(codes, scales, woven, lo, end):
             nc.vector.quantize_mx(
-                out=codes[:, lo:hi_col].bitcast(E4M3), scales=scales[:, lo:hi_col], in_=woven[:, PACK * lo : PACK * hi_col]
+                out=codes[:, lo:end].bitcast(E4M3), scales=scales[:, lo:end], in_=woven[:, PACK * lo : PACK * end]
             )
 
-        peak_order = (2, 0, 1, 3)
-
-        def product_pass(a, t, bank, lo, hi_col, opens, closes):
-            col = a * R + t * P
-            nc.tensor.matmul_mx(
-                out=bank,
-                lhsT=w_dealt[:, 2 * col : 2 * (col + P)].bitcast(E2M1),
-                lhsT_scale=ws_dealt[:, col : col + P],
-                rhs=u_codes[a][:, lo:hi_col].bitcast(E4M3),
-                rhs_scale=u_scales[a][:, lo:hi_col],
-                start=(a == 0 and opens),
-                stop=(a == PASSES - 1 and closes),
-            )
-
-        def first_product(a):
-            product_pass(a, 3, acc_head[:], 0, SL, True, True)
-            for t in peak_order[:3]:
-                product_pass(a, t, acc[t][:, 0:WIDE], 0, WIDE, True, False)
-                product_pass(a, t, acc[t][:, WIDE:J], WIDE, J, False, True)
-            product_pass(a, 3, acc[3][:, SL:J], SL, J, True, True)
-
-        for i in range(PLANES - 1):
-            gather_second(i, 0, J)
-            gather_first(i, FUSED, J)
-            gather_subtract(i, 0, FUSED)
-            subtract(i, FUSED, J)
-            scale_round(i, 0, FUSED)
-            scale_round(i, FUSED, J)
-            if i == 0:
-                nc.vector.tensor_copy(
-                    w_dealt[:].bitcast(U16).rearrange("p (a t m) -> p a t m", a=PASSES, t=PACK),
-                    w_raw[:].bitcast(U16).rearrange("p (a m t) -> p a t m", a=PASSES, t=PACK),
+        def first_product(a, codes, w_scale_plane):
+            def one_pass(t, bank, lo, end, opens, closes):
+                col = a * R + t * P
+                nc.tensor.matmul_mx(
+                    out=bank,
+                    lhsT=w_dealt[:, 2 * col : 2 * (col + P)].bitcast(E2M1),
+                    lhsT_scale=w_scale_plane[:, col : col + P],
+                    rhs=codes[:, lo:end].bitcast(E4M3),
+                    rhs_scale=u_scales[a][:, lo:end],
+                    start=(a == 0 and opens),
+                    stop=(a == PASSES - 1 and closes),
                 )
-            if i == 1:
-                nc.vector.tensor_copy(
-                    ws_dealt[:].rearrange("p (a t m) -> p a t m", a=PASSES, t=PACK),
-                    ws_raw[:].rearrange("p (a m t) -> p a t m", a=PASSES, t=PACK),
-                )
-            if i == PACK - 1:
-                weave(u_woven[0], u_pairs[0], 0, J)
-            if i == PACK + 1:
-                u_codes[0] = sb.tile([P, J], U32, name="u_codes0", tag="second%d" % i, align_bytes=64)
-                quantise(u_codes[0], u_scales[0], u_woven[0], 0, J)
-                first_product(0)
+
+            one_pass(3, acc_head[:], 0, SLICE, True, True)
+            for t in PEAK_ORDER[:-1]:
+                one_pass(t, acc[t][:, 0:WIDE], 0, WIDE, True, False)
+                one_pass(t, acc[t][:, WIDE:J], WIDE, J, False, True)
+            one_pass(3, acc[3][:, SLICE:J], SLICE, J, True, True)
 
         last = PLANES - 1
-        gather_second(last, 0, SL)
-        gather_subtract(last, 0, SL)
-        for s in range(1, SLICES):
-            gather_second(last, s * SL, (s + 1) * SL)
-            gather_first(last, s * SL, (s + 1) * SL)
-            subtract(last, s * SL, (s + 1) * SL)
-        for s in range(SLICES):
-            scale_round(last, s * SL, (s + 1) * SL)
-        for lo, hi_col in ((0, WIDE), (WIDE, J)):
-            weave(u_woven[1], u_pairs[1], lo, hi_col)
-        for lo, hi_col in ((0, WIDE), (WIDE, J)):
-            quantise(u_codes[1], u_scales[1], u_woven[1], lo, hi_col)
-        first_product(1)
+        for i in range(last):
+            fused = FUSED[i // PACK]
+            gather_second(i, 0, J)
+            gather_first(i, fused, J)
+            gather_subtract(i, 0, fused)
+            subtract(i, fused, J)
+            scale_round(i, 0, fused)
+            scale_round(i, fused, J)
+            if i == 0:
+                deal_columns(w_dealt[:].bitcast(U16), w_raw[:].bitcast(U16))
+            if i == PACK - 1:
+                ws_dealt = sb.tile([P, PASSES * R], U8, name="ws_dealt", tag="second%d" % i, align_bytes=64)
+                deal_columns(ws_dealt[:], ws_raw[:])
+                weave(u_woven[0], u_pairs[0], 0, J)
+            if i == PACK + 1:
+                u_codes_first = sb.tile([P, J], U32, name="u_codes0", tag="second%d" % i, align_bytes=64)
+                quantise(u_codes_first, u_scales[0], u_woven[0], 0, J)
+                first_product(0, u_codes_first, ws_dealt)
+
+        for lo in range(0, WIDE, SLICE):
+            gather_second(last, lo, lo + SLICE)
+            gather_subtract(last, lo, lo + SLICE)
+        gather_second(last, WIDE, J)
+        gather_first(last, WIDE, J)
+        subtract(last, WIDE, J)
+        for lo in range(0, J, SLICE):
+            scale_round(last, lo, lo + SLICE)
+        for lo, end in ((0, WIDE), (WIDE, J)):
+            weave(u_woven[1], u_pairs[1], lo, end)
+        for lo, end in ((0, WIDE), (WIDE, J)):
+            quantise(u_codes_last, u_scales[1], u_woven[1], lo, end)
+        first_product(1, u_codes_last, ws_dealt)
 
         scaled = [sb.tile([P, J], F32, name="scaled%d" % t) for t in range(PACK)]
         cut = [sb.tile([P, 1], F32, name="cut%d" % t) for t in range(PACK)]
@@ -200,44 +211,52 @@ def tile_list_pickgaps_peakgated_capped_kernel(tc, xf, fk, w_words, w_scales, wb
         h_codes = sb.tile([P, J], U32, name="h_codes", align_bytes=64)
         h_scales = sb.tile([P, J], U8, name="h_scales", align_bytes=64)
         cut_head = sb.tile([P, 1], F32, name="cut_head")
-        nc.vector.tensor_scalar(scaled[3][:, 0:SL], acc_head[:], -0.4, None, ALU.mult, ALU.min, accum_out=cut_head[:])
-        for t in peak_order[:3]:
-            nc.vector.tensor_scalar(scaled[t][:], acc[t][:], -0.4, None, ALU.mult, ALU.min, accum_out=cut[t][:])
-            lo = 0 if t < 2 else SL
+        nc.vector.tensor_scalar(
+            scaled[3][:, 0:SLICE], acc_head[:], -PEAK_SHARE, None, ALU.mult, ALU.min, accum_out=cut_head[:]
+        )
+        for t in PEAK_ORDER[:-1]:
+            nc.vector.tensor_scalar(scaled[t][:], acc[t][:], -PEAK_SHARE, None, ALU.mult, ALU.min, accum_out=cut[t][:])
+            lo = 0 if t < 2 else SLICE
             nc.scalar.activation(pair_view(h_pairs, t, lo, J), acc[t][:, lo:J], ACT.Relu, bias=cut[t][:])
-        nc.vector.tensor_scalar(scaled[3][:, SL:J], acc[3][:, SL:J], -0.4, cut_head[:], ALU.mult, ALU.min, accum_out=cut[3][:])
-        nc.vector.tensor_scalar(pair_view(h_pairs, 2, 0, SL), acc[2][:, 0:SL], cut[2][:], 0.0, ALU.add, ALU.max)
-        nc.vector.tensor_scalar(pair_view(h_pairs, 3, 0, SL), acc_head[:], cut[3][:], 0.0, ALU.add, ALU.max)
-        for s in range(1, SLICES):
+        nc.vector.tensor_scalar(
+            scaled[3][:, SLICE:J], acc[3][:, SLICE:J], -PEAK_SHARE, cut_head[:], ALU.mult, ALU.min, accum_out=cut[3][:]
+        )
+        nc.vector.tensor_scalar(pair_view(h_pairs, 2, 0, SLICE), acc[2][:, 0:SLICE], cut[2][:], 0.0, ALU.add, ALU.max)
+        nc.vector.tensor_scalar(pair_view(h_pairs, 3, 0, SLICE), acc_head[:], cut[3][:], 0.0, ALU.add, ALU.max)
+        for lo in range(SLICE, J, SLICE):
             nc.scalar.activation(
-                pair_view(h_pairs, 3, s * SL, (s + 1) * SL), acc[3][:, s * SL : (s + 1) * SL], ACT.Relu, bias=cut[3][:]
+                pair_view(h_pairs, 3, lo, lo + SLICE), acc[3][:, lo : lo + SLICE], ACT.Relu, bias=cut[3][:]
             )
 
-        prod = [ps.tile([P, N // P, SL], F32, name="prod%d" % s) for s in range(SLICES)]
-        under = [sb.tile([P, N // P, SL], F32, name="under%d" % s) for s in range(SLICES)]
-        result = [sb.tile([P, N // P, SL], F32, name="result%d" % s) for s in range(SLICES)]
+        prod = [ps.tile([P, OUT_TILES, SLICE], F32, name="prod%d" % s) for s in range(SLICES)]
+        under = [sb.tile([P, OUT_TILES, SLICE], F32, name="under%d" % s) for s in range(SLICES)]
+        result = [sb.tile([P, OUT_TILES, SLICE], F32, name="result%d" % s) for s in range(SLICES)]
         out_rows = out.rearrange("(c p) j -> p c j", p=P)
-        slice_order = (0, 1, 2)
-        for s in slice_order:
-            weave(h_woven, h_pairs, s * SL, (s + 1) * SL)
-        for s in slice_order:
-            lo, hi_col = s * SL, (s + 1) * SL
-            quantise(h_codes, h_scales, h_woven, lo, hi_col)
-            for c in range(N // P):
+        for s in range(SLICES):
+            weave(h_woven, h_pairs, s * SLICE, (s + 1) * SLICE)
+        for s in range(SLICES):
+            lo, end = s * SLICE, (s + 1) * SLICE
+            quantise(h_codes, h_scales, h_woven, lo, end)
+            for c in range(OUT_TILES):
                 nc.tensor.matmul_mx(
                     out=prod[s][:, c, :],
                     lhsT=wb[:, c * P : (c + 1) * P].bitcast(E5M2),
                     lhsT_scale=wbs[:, c * P : (c + 1) * P],
-                    rhs=h_codes[:, lo:hi_col].bitcast(E4M3),
-                    rhs_scale=h_scales[:, lo:hi_col],
+                    rhs=h_codes[:, lo:end].bitcast(E4M3),
+                    rhs_scale=h_scales[:, lo:end],
                     start=True,
                     stop=True,
                 )
-        for s in slice_order:
-            lo, hi_col = s * SL, (s + 1) * SL
-            for c in range(N // P):
+        for s in range(SLICES):
+            lo, end = s * SLICE, (s + 1) * SLICE
+            for c in range(OUT_TILES):
                 nc.scalar.activation(under[s][:, c, :], prod[s][:, c, :], ACT.Relu, bias=hi_sb[:, c : c + 1], scale=-1.0)
             nc.vector.scalar_tensor_tensor(
-                result[s][:], under[s][:], -1.0, rw_sb[:, lo:hi_col].unsqueeze(1).to_broadcast([P, N // P, SL]), ALU.mult, ALU.mult
+                result[s][:],
+                under[s][:],
+                -1.0,
+                rw_sb[:, lo:end].unsqueeze(1).to_broadcast([P, OUT_TILES, SLICE]),
+                ALU.mult,
+                ALU.mult,
             )
-            nc.sync.dma_start(out_rows[:, :, lo:hi_col], result[s][:])
+            nc.sync.dma_start(out_rows[:, :, lo:end], result[s][:])

from contextlib import ExitStack

import concourse.mybir as mybir

K, T, J, R, N = 1024, 1024, 384, 512, 256
FLOPS = 2 * K * R * J + 2 * R * N * J

F32 = mybir.dt.float32
BF16 = mybir.dt.bfloat16
I32 = mybir.dt.int32
U32 = mybir.dt.uint32
U16 = mybir.dt.uint16
U8 = mybir.dt.uint8
E4M3 = mybir.dt.float8_e4m3fn_x4
E5M2 = mybir.dt.float8_e5m2_x4
E2M1 = mybir.dt.float4_e2m1fn_x4
ALU = mybir.AluOpType
ACT = mybir.ActivationFunctionType

P = 128
PACK = 4
PASSES = K // (P * PACK)
PLANES = PASSES * PACK
QUADRANTS = 4
ENTRIES_PER_COLUMN = 16
SLICE = 128
SLICES = J // SLICE
WIDE = 2 * SLICE
OUT_TILES = N // P
PEAK_SHARE = 0.4

FUSED = (256, 128)

PEAK_ORDER = (2, 0, 1, 3)


def tile_list_pickgaps_peakgated_capped_kernel(
    tc, xf, fk, w_words, w_scales, wb_words, wb_scales, hi, rw, offs, offs2, out
):
    nc = tc.nc
    with ExitStack() as ctx:
        sb = ctx.enter_context(tc.tile_pool(name="sb", bufs=1))
        ps = ctx.enter_context(tc.psum_pool(name="ps", bufs=1))

        list1 = sb.tile([P, J // ENTRIES_PER_COLUMN], U16, name="list1")
        list2 = sb.tile([P, J // ENTRIES_PER_COLUMN], U16, name="list2")
        x = [sb.tile([P, T], F32, name="x%d" % i) for i in range(PLANES)]
        w_raw = sb.tile([P, PASSES * 2 * R], U8, name="w_raw")
        ws_raw = sb.tile([P, PASSES * R], U8, name="ws_raw")
        w_dealt = sb.tile([P, PASSES * 2 * R], U8, name="w_dealt", align_bytes=64)
        wb = sb.tile([P, N], I32, name="wb", align_bytes=64)
        wbs = sb.tile([P, N], U8, name="wbs", align_bytes=64)
        fk_sb = [sb.tile([P, PACK], F32, name="fk_sb%d" % a) for a in range(PASSES)]
        hi_sb = sb.tile([P, OUT_TILES], F32, name="hi_sb")
        rw_sb = sb.tile([P, J], F32, name="rw_sb")

        nc.vector.memset(ws_raw[:].bitcast(U32), 0)
        nc.vector.memset(wbs[:].bitcast(U32), 0)

        warm_in = sb.tile([P, 1], F32, name="warm_in")
        warm_out = sb.tile([P, 1], F32, name="warm_out")
        nc.gpsimd.memset(warm_in[:], 0.0)
        nc.scalar.activation(warm_out[:], warm_in[:], ACT.Copy)

        x_rows = xf.rearrange("(a p t) c -> a t p c", p=P, t=PACK)

        def load_plane(i):
            nc.sync.dma_start(x[i][:], x_rows[i // PACK, i % PACK])

        fk_rows = fk.rearrange("(a p t) o -> a p (t o)", p=P, t=PACK)
        nc.sync.dma_start(list2[:], offs2)
        load_plane(0)
        nc.sync.dma_start(list1[:], offs)
        nc.sync.dma_start(fk_sb[0][:], fk_rows[0])
        nc.sync.dma_start(
            w_raw[:].bitcast(I32).rearrange("p (a c) -> p a c", a=PASSES),
            w_words.bitcast(I32).rearrange("a p c -> p a c"),
        )
        load_plane(1)
        load_plane(2)
        ws_rows = w_scales.bitcast(I32).rearrange("a q c -> q a c")
        for q in range(QUADRANTS):
            nc.sync.dma_start(
                ws_raw[32 * q : 32 * q + 4, :].bitcast(I32).rearrange("p (a c) -> p a c", a=PASSES),
                ws_rows[4 * q : 4 * q + 4],
            )
        load_plane(3)
        nc.sync.dma_start(fk_sb[1][:], fk_rows[1])
        for i in range(PACK, PLANES):
            load_plane(i)
        nc.sync.dma_start(wb[:], wb_words[0].rearrange("p n t -> p (n t)").bitcast(I32))
        for q in range(QUADRANTS):
            nc.sync.dma_start(wbs[32 * q : 32 * q + 4, :].bitcast(I32), wb_scales[0].bitcast(I32)[4 * q : 4 * q + 4, :])
        with nc.allow_non_contiguous_dma(reason="one bound for each partition"):
            nc.sync.dma_start(hi_sb[:], hi.rearrange("(c p) o -> p (c o)", p=P))
        nc.sync.dma_start(rw_sb[:], rw[0].partition_broadcast(P))

        second = [
            sb.tile([P, J], F32, name="second%d" % i, tag="second%d" % i, align_bytes=64) for i in range(PLANES)
        ]
        first = [sb.tile([P, J], F32, name="first%d" % i) for i in range(PLANES)]
        gap = [sb.tile([P, J], F32, name="gap%d" % i) for i in range(PLANES)]
        u_pairs = [sb.tile([P, PACK * J], BF16, name="u_pairs%d" % a) for a in range(PASSES)]
        u_woven = [sb.tile([P, PACK * J], BF16, name="u_woven%d" % a, align_bytes=64) for a in range(PASSES)]
        u_codes_last = sb.tile([P, J], U32, name="u_codes1", align_bytes=64)
        u_scales = [sb.tile([P, J], U8, name="u_scales%d" % a, align_bytes=64) for a in range(PASSES)]
        acc = [ps.tile([P, J], F32, name="acc%d" % t) for t in range(PACK)]
        acc_head = ps.tile([P, SLICE], F32, name="acc_head")

        def entries(list_tile, lo, end):
            return list_tile[:, lo // ENTRIES_PER_COLUMN : end // ENTRIES_PER_COLUMN]

        def pair_view(pairs, t, lo, end):
            base = (t // 2) * 2 * J + t % 2
            return pairs[:, base + 2 * lo : base + 2 * end - 1 : 2]

        def gather_second(i, lo, end):
            nc.scalar.activation(second[i][:, lo:end], x[i][:].indirect(entries(list2, lo, end)), ACT.Copy)

        def gather_first(i, lo, end):
            nc.scalar.activation(first[i][:, lo:end], x[i][:].indirect(entries(list1, lo, end)), ACT.Copy)

        def gather_subtract(i, lo, end):
            nc.vector.tensor_tensor(
                gap[i][:, lo:end], x[i][:].indirect(entries(list1, lo, end)), second[i][:, lo:end], ALU.subtract
            )

        def subtract(i, lo, end):
            nc.vector.tensor_tensor(gap[i][:, lo:end], first[i][:, lo:end], second[i][:, lo:end], ALU.subtract)

        def scale_round(i, lo, end):
            a, t = divmod(i, PACK)
            nc.vector.tensor_scalar(
                pair_view(u_pairs[a], t, lo, end), gap[i][:, lo:end], fk_sb[a][:, t : t + 1], None, ALU.mult
            )

        def deal_columns(dealt, raw):
            nc.vector.tensor_copy(
                dealt.rearrange("p (a t m) -> p a t m", a=PASSES, t=PACK),
                raw.rearrange("p (a m t) -> p a t m", a=PASSES, t=PACK),
            )

        def weave(woven, pairs, lo, end):
            nc.vector.tensor_copy(
                woven[:].bitcast(I32)[:, 2 * lo : 2 * end].rearrange("p (j h) -> p j h", h=2),
                pairs[:].bitcast(I32).rearrange("p (h j) -> p j h", h=2)[:, lo:end],
            )

        def quantise(codes, scales, woven, lo, end):
            nc.vector.quantize_mx(
                out=codes[:, lo:end].bitcast(E4M3), scales=scales[:, lo:end], in_=woven[:, PACK * lo : PACK * end]
            )

        def first_product(a, codes, w_scale_plane):
            def one_pass(t, bank, lo, end, opens, closes):
                col = a * R + t * P
                nc.tensor.matmul_mx(
                    out=bank,
                    lhsT=w_dealt[:, 2 * col : 2 * (col + P)].bitcast(E2M1),
                    lhsT_scale=w_scale_plane[:, col : col + P],
                    rhs=codes[:, lo:end].bitcast(E4M3),
                    rhs_scale=u_scales[a][:, lo:end],
                    start=(a == 0 and opens),
                    stop=(a == PASSES - 1 and closes),
                )

            one_pass(3, acc_head[:], 0, SLICE, True, True)
            for t in PEAK_ORDER[:-1]:
                one_pass(t, acc[t][:, 0:WIDE], 0, WIDE, True, False)
                one_pass(t, acc[t][:, WIDE:J], WIDE, J, False, True)
            one_pass(3, acc[3][:, SLICE:J], SLICE, J, True, True)

        last = PLANES - 1
        for i in range(last):
            fused = FUSED[i // PACK]
            gather_second(i, 0, J)
            gather_first(i, fused, J)
            gather_subtract(i, 0, fused)
            subtract(i, fused, J)
            scale_round(i, 0, fused)
            scale_round(i, fused, J)
            if i == 0:
                deal_columns(w_dealt[:].bitcast(U16), w_raw[:].bitcast(U16))
            if i == PACK - 1:
                ws_dealt = sb.tile([P, PASSES * R], U8, name="ws_dealt", tag="second%d" % i, align_bytes=64)
                deal_columns(ws_dealt[:], ws_raw[:])
                weave(u_woven[0], u_pairs[0], 0, J)
            if i == PACK + 1:
                u_codes_first = sb.tile([P, J], U32, name="u_codes0", tag="second%d" % i, align_bytes=64)
                quantise(u_codes_first, u_scales[0], u_woven[0], 0, J)
                first_product(0, u_codes_first, ws_dealt)

        for lo in range(0, WIDE, SLICE):
            gather_second(last, lo, lo + SLICE)
            gather_subtract(last, lo, lo + SLICE)
        gather_second(last, WIDE, J)
        gather_first(last, WIDE, J)
        subtract(last, WIDE, J)
        for lo in range(0, J, SLICE):
            scale_round(last, lo, lo + SLICE)
        for lo, end in ((0, WIDE), (WIDE, J)):
            weave(u_woven[1], u_pairs[1], lo, end)
        for lo, end in ((0, WIDE), (WIDE, J)):
            quantise(u_codes_last, u_scales[1], u_woven[1], lo, end)
        first_product(1, u_codes_last, ws_dealt)

        scaled = [sb.tile([P, J], F32, name="scaled%d" % t) for t in range(PACK)]
        cut = [sb.tile([P, 1], F32, name="cut%d" % t) for t in range(PACK)]
        h_pairs = sb.tile([P, PACK * J], BF16, name="h_pairs")
        h_woven = sb.tile([P, PACK * J], BF16, name="h_woven", align_bytes=64)
        h_codes = sb.tile([P, J], U32, name="h_codes", align_bytes=64)
        h_scales = sb.tile([P, J], U8, name="h_scales", align_bytes=64)
        cut_head = sb.tile([P, 1], F32, name="cut_head")
        nc.vector.tensor_scalar(
            scaled[3][:, 0:SLICE], acc_head[:], -PEAK_SHARE, None, ALU.mult, ALU.min, accum_out=cut_head[:]
        )
        for t in PEAK_ORDER[:-1]:
            nc.vector.tensor_scalar(scaled[t][:], acc[t][:], -PEAK_SHARE, None, ALU.mult, ALU.min, accum_out=cut[t][:])
            lo = 0 if t < 2 else SLICE
            nc.scalar.activation(pair_view(h_pairs, t, lo, J), acc[t][:, lo:J], ACT.Relu, bias=cut[t][:])
        nc.vector.tensor_scalar(
            scaled[3][:, SLICE:J], acc[3][:, SLICE:J], -PEAK_SHARE, cut_head[:], ALU.mult, ALU.min, accum_out=cut[3][:]
        )
        nc.vector.tensor_scalar(pair_view(h_pairs, 2, 0, SLICE), acc[2][:, 0:SLICE], cut[2][:], 0.0, ALU.add, ALU.max)
        nc.vector.tensor_scalar(pair_view(h_pairs, 3, 0, SLICE), acc_head[:], cut[3][:], 0.0, ALU.add, ALU.max)
        for lo in range(SLICE, J, SLICE):
            nc.scalar.activation(
                pair_view(h_pairs, 3, lo, lo + SLICE), acc[3][:, lo : lo + SLICE], ACT.Relu, bias=cut[3][:]
            )

        prod = [ps.tile([P, OUT_TILES, SLICE], F32, name="prod%d" % s) for s in range(SLICES)]
        under = [sb.tile([P, OUT_TILES, SLICE], F32, name="under%d" % s) for s in range(SLICES)]
        result = [sb.tile([P, OUT_TILES, SLICE], F32, name="result%d" % s) for s in range(SLICES)]
        out_rows = out.rearrange("(c p) j -> p c j", p=P)
        for s in range(SLICES):
            weave(h_woven, h_pairs, s * SLICE, (s + 1) * SLICE)
        for s in range(SLICES):
            lo, end = s * SLICE, (s + 1) * SLICE
            quantise(h_codes, h_scales, h_woven, lo, end)
            for c in range(OUT_TILES):
                nc.tensor.matmul_mx(
                    out=prod[s][:, c, :],
                    lhsT=wb[:, c * P : (c + 1) * P].bitcast(E5M2),
                    lhsT_scale=wbs[:, c * P : (c + 1) * P],
                    rhs=h_codes[:, lo:end].bitcast(E4M3),
                    rhs_scale=h_scales[:, lo:end],
                    start=True,
                    stop=True,
                )
        for s in range(SLICES):
            lo, end = s * SLICE, (s + 1) * SLICE
            for c in range(OUT_TILES):
                nc.scalar.activation(under[s][:, c, :], prod[s][:, c, :], ACT.Relu, bias=hi_sb[:, c : c + 1], scale=-1.0)
            nc.vector.scalar_tensor_tensor(
                result[s][:],
                under[s][:],
                -1.0,
                rw_sb[:, lo:end].unsqueeze(1).to_broadcast([P, OUT_TILES, SLICE]),
                ALU.mult,
                ALU.mult,
            )
            nc.sync.dma_start(out_rows[:, :, lo:end], result[s][:])
